import numpy as np
import ml_dtypes


def mxq(x, axis, fmt="e4m3"):
    dtype, down = {"e4m3": (ml_dtypes.float8_e4m3fn, 7), "e5m2": (ml_dtypes.float8_e5m2, 14)}[fmt]
    v = np.moveaxis(np.asarray(x, np.float32).astype(ml_dtypes.bfloat16).astype(np.float64), axis, -1)
    blocks = v.reshape(v.shape[:-1] + (-1, 32))
    amax = np.abs(blocks).max(-1, keepdims=True)
    byte = np.maximum(np.where(amax > 0, np.frexp(amax)[1] - 1 + 127, 0) - down, 1)
    scale = np.exp2(byte - 127.0)
    codes = (blocks / scale).astype(np.float32).astype(dtype).astype(np.float64)
    return np.moveaxis((codes * scale).reshape(v.shape), -1, axis)


WIDE = False


def mx_kscale(k):
    if not WIDE:
        return np.ones(k)
    levels = np.array([10, -10, 5, -5, 0])
    if k % 512:
        return np.exp2(np.random.permutation(np.resize(levels, k // 32))).repeat(32)
    a = np.empty((k // 512, 16))
    for p in range(k // 512):
        a[p, :8] = np.random.permutation(np.resize(levels, 8))
        for g in range(8):
            far = levels[np.abs(levels - a[p, g]) >= 10]
            a[p, g + 8] = far[np.random.randint(len(far))]
    return np.exp2(a.ravel()).repeat(32)


def f64(x):
    return np.asarray(x).astype(np.float64)


def striped(idx):
    return np.tile(idx.reshape(-1, 16).T, (8, 1)).astype(np.uint16)


def unstriped(offs):
    return offs[:16].T.reshape(-1).astype(np.int64)


E2M1 = np.array([0.0, 0.5, 1.0, 1.5, 2.0, 3.0, 4.0, 6.0, -0.0, -0.5, -1.0, -1.5, -2.0, -3.0, -4.0, -6.0])


def pack_weight(w, fmt):
    k, n = w.shape
    w = f64(np.asarray(w, np.float32).astype(ml_dtypes.bfloat16)).reshape(k // 32, 32, n)
    amax = np.abs(w).max(1)
    if fmt == "e4m3":
        byte = np.frexp(amax)[1] - 1 + 127 - 7
    else:
        mant, ex = np.frexp(amax / 6.0)
        byte = np.where(mant > 0.5, ex, ex - 1) + 127
    byte = np.clip(np.where(amax > 0, byte, 1), 1, 254)
    scaled = (w * np.exp2(127.0 - byte)[:, None, :]).reshape(k, n).astype(np.float32)
    by_word = np.ascontiguousarray(scaled.reshape(k // 512, 128, 4, n).transpose(0, 1, 3, 2))
    if fmt == "e4m3":
        words = by_word.astype(ml_dtypes.float8_e4m3fn).view(np.uint8)
    else:
        c = by_word.astype(ml_dtypes.float4_e2m1fn).view(np.uint8) & 0xF
        words = (c[..., 0::2] | (c[..., 1::2] << 4)).reshape(k // 512, 128, 2 * n)
    return np.ascontiguousarray(words), np.ascontiguousarray(byte.astype(np.uint8).reshape(k // 512, 16, n))


def unpack_weight(words, scales, fmt):
    g, _, n = scales.shape
    words = np.ascontiguousarray(words).reshape(g, 128, n, -1)
    if fmt == "e4m3":
        vals = words.view(ml_dtypes.float8_e4m3fn).astype(np.float64)
    else:
        nib = np.empty((g, 128, n, 4), np.uint8)
        nib[..., 0::2] = words & 0xF
        nib[..., 1::2] = words >> 4
        vals = E2M1[nib]
    vals = vals * np.repeat(np.exp2(scales.astype(np.float64) - 127.0), 8, axis=1)[..., None]
    return vals.transpose(0, 1, 3, 2).reshape(g * 512, n)


def gelu(v):
    return 0.5 * v * (1.0 + np.tanh(np.sqrt(2.0 / np.pi) * (v + 0.044715 * v**3)))


def bf(x):
    return np.asarray(x, np.float32).astype(ml_dtypes.bfloat16)

def planes(Y):
    n, m = Y.shape
    b = f64(bf(Y)).reshape(n // 32, 32, m)
    amax = np.abs(b).max(1)
    byte = np.clip(np.where(amax > 0, np.frexp(amax)[1] - 1 + 127 - 7, 1), 1, 254)
    codes = (b * np.exp2(127.0 - byte)[:, None, :]).reshape(n, m).astype(np.float32).astype(ml_dtypes.float8_e4m3fn).view(np.uint8)
    words = codes.reshape(n // 512, 128, 4, m).transpose(0, 1, 3, 2)
    return np.ascontiguousarray(words), np.ascontiguousarray(byte.astype(np.uint8).reshape(n // 512, 16, m))


K, T, S, H, N = 512, 2048, 1024, 1024, 1024


def setup_inputs():
    n = np.random.standard_normal
    s = mx_kscale(K)[:, None]
    u = mx_kscale(H)
    tab_words, tab_scales = pack_weight(n((K, T)) * s, "e4m3")
    wa = 0.33 * n((K, H)) / np.sqrt(K) / s
    w4_words, w4_scales = pack_weight(1.3 * n((H, N)) / np.sqrt(H) / u[:, None], "e2m1")
    return {
        "tab_words": tab_words,
        "tab_scales": tab_scales,
        "offs": striped(np.random.permutation(T)[:S]),
        "wa": wa.astype(np.float32),
        "gT": np.random.uniform(0.5, 1.5, (H, T)).astype(np.float32),
        "gain": (np.exp(0.3 * n(H)) * u).astype(np.float32),
        "w4_words": w4_words,
        "w4_scales": w4_scales,
        "amp": np.exp(0.8 * n(N)).astype(np.float32),
    }


def reference(tab_words, tab_scales, offs, wa, gT, gain, w4_words, w4_scales, amp):
    v = unpack_weight(tab_words, tab_scales, "e4m3")[:, unstriped(offs)]
    g = f64(gT)[:, unstriped(offs)]
    a = mxq(f64(wa), 0, "e4m3").T @ v
    h = f64(gain)[:, None] * np.sin(a * g)
    w4 = unpack_weight(w4_words, w4_scales, "e2m1")
    phase = w4.T @ mxq(h, 0, "e4m3")
    y = f64(amp)[:, None] * np.sin(phase)
    words, scales = planes(y)
    return y, words, scales

@@ -1,0 +1,245 @@
+from contextlib import ExitStack
+
+import concourse.mybir as mybir
+
+K, T, S, H, N = 512, 2048, 1024, 1024, 1024
+FLOPS = 2 * K * H * S + 2 * H * N * S
+
+F32 = mybir.dt.float32
+BF16 = mybir.dt.bfloat16
+I32 = mybir.dt.int32
+U32 = mybir.dt.uint32
+U16 = mybir.dt.uint16
+U8 = mybir.dt.uint8
+FP8X4 = mybir.dt.float8_e4m3fn_x4
+FP4X4 = mybir.dt.float4_e2m1fn_x4
+MULT = mybir.AluOpType.mult
+ADD = mybir.AluOpType.add
+SIN = mybir.ActivationFunctionType.Sin
+COPY = mybir.ActivationFunctionType.Copy
+
+P = 128
+W = 512
+
+
+def tile_list_implicit_audio_sines_kernel(
+    tc, tab_words, tab_scales, offs, wa, gT, gain, w4_words, w4_scales, amp, out_0, out_1, out_2
+):
+    nc = tc.nc
+    with ExitStack() as ctx:
+        keep = ctx.enter_context(tc.tile_pool(name="keep", bufs=1))
+        ring = ctx.enter_context(tc.tile_pool(name="ring", bufs=4))
+        wide = ctx.enter_context(tc.tile_pool(name="wide", bufs=2))
+        psum = ctx.enter_context(tc.psum_pool(name="psum", bufs=8))
+
+        offsets = keep.tile([P, S // 16], U16, name="offsets")
+        tabw = keep.tile([P, T], I32, name="tabw", align_bytes=64)
+        tabs = keep.tile([P, T], U8, name="tabs", align_bytes=64)
+        wa_raw = [keep.tile([P, 4, 512], F32, name=f"wa_raw{b}", tag="big", bufs=4) for b in range(2)]
+        freq = [keep.tile([P, T], F32, name=f"freq{s}") for s in range(8)]
+        w4_raw = keep.tile([P, 2, N // 2], I32, name="w4_raw", align_bytes=64)
+        w4s_raw = keep.tile([P, 2, N], U8, name="w4s_raw", align_bytes=64)
+        gain_sb = keep.tile([P, 2, 4], F32, name="gain_sb")
+        amp_sb = keep.tile([P, 2, 4], F32, name="amp_sb")
+
+        nc.vector.memset(tabs[:].bitcast(I32), 0)
+        nc.gpsimd.memset(w4s_raw[:].bitcast(I32), 0)
+
+        wa_rows = wa.rearrange("(p j) c -> p j c", j=4)
+        g_rows = gT.rearrange("(b p t) c -> b t p c", b=2, t=4)
+
+        def load_freq(s):
+            nc.sync.dma_start(out=freq[s][:], in_=g_rows[s // 4, s % 4])
+
+        def load_wa(b):
+            nc.sync.dma_start(out=wa_raw[b][:], in_=wa_rows[:, :, 512 * b : 512 * (b + 1)])
+
+        nc.sync.dma_start(offsets[:], offs)
+        load_wa(0)
+        for q in range(4):
+            nc.sync.dma_start(
+                out=tabs[32 * q : 32 * q + 4, :].bitcast(I32), in_=tab_scales[0, 4 * q : 4 * q + 4, :].bitcast(I32)
+            )
+        nc.sync.dma_start(out=tabw[:], in_=tab_words[0].rearrange("p n t -> p (n t)").bitcast(I32))
+        for q in range(4):
+            nc.gpsimd.dma_start(
+                out=w4s_raw[32 * q : 32 * q + 4].bitcast(I32),
+                in_=w4_scales[:, 4 * q : 4 * q + 4, :].rearrange("a r c -> r a c").bitcast(I32),
+            )
+        load_freq(0)
+        nc.sync.dma_start(out=gain_sb[:], in_=gain.rearrange("(b p t) -> p b t", b=2, t=4))
+        load_freq(1)
+        load_wa(1)
+        load_freq(2)
+        load_freq(3)
+        load_freq(4)
+        load_freq(5)
+        load_freq(6)
+        load_freq(7)
+        nc.sync.dma_start(out=w4_raw[:], in_=w4_words.rearrange("a p c -> p a c").bitcast(I32))
+        nc.sync.dma_start(out=amp_sb[:], in_=amp.rearrange("(g p t) -> p g t", g=2, t=4))
+
+        v_codes = [keep.tile([P, W], U32, name=f"v_codes{h}", align_bytes=64) for h in range(2)]
+        v_scales = [keep.tile([P, W], U8, name=f"v_scales{h}", align_bytes=64) for h in range(2)]
+        wa_codes = [keep.tile([P, 512], U32, name=f"wa_codes{b}", align_bytes=64) for b in range(2)]
+        wa_scales = [keep.tile([P, 512], U8, name=f"wa_scales{b}", align_bytes=64) for b in range(2)]
+        w4_codes = keep.tile([P, 2, 2 * N], U8, name="w4_codes", align_bytes=64)
+        w4_planes = keep.tile([P, 2, N], U8, name="w4_planes", align_bytes=64)
+        h_codes = {}
+        h_scales = {}
+        for b in range(2):
+            for h in range(2):
+                h_codes[b, h] = keep.tile([P, W], U32, name=f"h_codes{b}{h}", align_bytes=64)
+                h_scales[b, h] = keep.tile([P, W], U8, name=f"h_scales{b}{h}", align_bytes=64)
+        y_scales = [keep.tile([P, 2, W], U8, name=f"y_scales{h}", align_bytes=64) for h in range(2)]
+
+        def half_list(h):
+            return offsets[:, h * (W // 16) : (h + 1) * (W // 16)]
+
+        def look_up_codes(h):
+            nc.vector.tensor_copy(out=v_codes[h][:], in_=tabw[:].bitcast(U32).indirect(half_list(h)))
+            nc.vector.tensor_copy(out=v_scales[h][:], in_=tabs[:].indirect(half_list(h)))
+
+        def quantise_wa(b):
+            grouped = wide.tile([P, 4, P, 4], BF16, name="wa_grouped", align_bytes=64)
+            (nc.vector.tensor_copy if ("v" if b else "s") == "v" else nc.scalar.copy)(
+                out=grouped[:].rearrange("p t m j -> p m j t"),
+                in_=wa_raw[b][:].rearrange("p j (m t) -> p m j t", t=4),
+            )
+            nc.vector.quantize_mx(
+                out=wa_codes[b][:].bitcast(FP8X4),
+                scales=wa_scales[b][:],
+                in_=grouped[:].rearrange("p t m j -> p (t m j)"),
+            )
+
+        def deal_w4():
+            nc.vector.tensor_copy(
+                out=w4_codes[:].bitcast(U16).rearrange("p a (g t m) -> p (a g) t m", g=2, t=4),
+                in_=w4_raw[:].bitcast(U16).rearrange("p a (g m t) -> p (a g) t m", g=2, t=4),
+            )
+            nc.vector.tensor_copy(
+                out=w4_planes[:].rearrange("p a (g t m) -> p (a g) t m", g=2, t=4),
+                in_=w4s_raw[:].rearrange("p a (g m t) -> p (a g) t m", g=2, t=4),
+            )
+
+        def interleave(eng, dst, src):
+            d = dst.rearrange("p (c i) t -> p c t i", i=4)
+            s = src.rearrange("p t (c i) -> p c t i", i=4)
+            if eng == "v":
+                nc.vector.tensor_copy(out=d, in_=s)
+            elif eng == "s":
+                nc.scalar.copy(out=d, in_=s)
+            else:
+                nc.gpsimd.tensor_scalar(out=d, in0=s, scalar1=1.0, scalar2=0.0, op0=MULT, op1=ADD)
+
+        def scale_rows(eng, dst, src, col):
+            if eng == "v":
+                nc.vector.tensor_scalar(out=dst, in0=src, scalar1=col, scalar2=None, op0=MULT)
+            elif eng == "s":
+                nc.scalar.activation(out=dst, in_=src, func=COPY, scale=col)
+            else:
+                nc.gpsimd.tensor_scalar(out=dst, in0=src, scalar1=col, scalar2=0.0, op0=MULT, op1=ADD)
+
+        h_rows = {}
+
+        slots = [keep.tile([P, W], F32, name=f"slot{i}") for i in range(12)]
+        steps = [(0, t, h) for t in range(4) for h in range(2)] + [(1, t, h) for h in range(2) for t in range(4)]
+
+        def project(i):
+            b, t, h = steps[i]
+            acc = psum.tile([P, W], F32, name="acc")
+            cols = slice(P * t, P * (t + 1))
+            nc.tensor.matmul_mx(
+                out=acc[:],
+                lhsT=wa_codes[b][:, cols].bitcast(FP8X4),
+                lhsT_scale=wa_scales[b][:, cols],
+                rhs=v_codes[h][:].bitcast(FP8X4),
+                rhs_scale=v_scales[h][:],
+                start=True,
+                stop=True,
+            )
+            nc.scalar.copy(out=slots[(i + 2) % 12][:], in_=acc[:])
+
+        def modulate(i):
+            b, t, h = steps[i]
+            if t == 0:
+                h_rows[b, h] = wide.tile([P, 4, W], BF16, name="h_rows", bufs=2)
+            proj = slots[(i + 2) % 12]
+            phase = slots[(i + 0) % 12]
+            nc.vector.tensor_tensor(out=phase[:], in0=freq[4 * b + t][:].indirect(half_list(h)), in1=proj[:], op=MULT)
+            sine = ring.tile([P, W], F32, name="sine")
+            nc.scalar.activation(out=sine[:], in_=phase[:], func=SIN)
+            scale_rows("v" if i >= 14 else "s", h_rows[b, h][:, t, :], sine[:], gain_sb[:, b, t : t + 1])
+
+        def quantise_h(b, h):
+            grouped = wide.tile([P, W, 4], BF16, name="h_grouped", align_bytes=64)
+            interleave("v", grouped[:], h_rows[b, h][:])
+            nc.vector.quantize_mx(
+                out=h_codes[b, h][:].bitcast(FP8X4),
+                scales=h_scales[b, h][:],
+                in_=grouped[:].rearrange("p j t -> p (j t)"),
+            )
+
+        y_rows = {}
+        y_out = out_0.rearrange("(g p t) j -> g p t j", g=2, t=4)
+
+        def second_slice(g, t, h):
+            if t == 0:
+                y_rows[g, h] = keep.tile([P, 4, W], F32, name=f"y_rows{g}{h}", tag="big", bufs=4)
+            acc = psum.tile([P, W], F32, name="acc")
+            c0 = 512 * g + P * t
+            for b in range(2):
+                nc.tensor.matmul_mx(
+                    out=acc[:],
+                    lhsT=w4_codes[:, b, 2 * c0 : 2 * (c0 + P)].bitcast(FP4X4),
+                    lhsT_scale=w4_planes[:, b, c0 : c0 + P],
+                    rhs=h_codes[b, h][:].bitcast(FP8X4),
+                    rhs_scale=h_scales[b, h][:],
+                    start=(b == 0),
+                    stop=(b == 1),
+                )
+            sine = ring.tile([P, W], F32, name="sine2")
+            nc.scalar.activation(out=sine[:], in_=acc[:], func=SIN)
+            scale_rows("s" if t == 0 else "v", y_rows[g, h][:, t, :], sine[:], amp_sb[:, g, t : t + 1])
+            nc.sync.dma_start(out=y_out[g, :, t, W * h : W * (h + 1)], in_=y_rows[g, h][:, t, :])
+
+        def quantise_y(g, h):
+            grouped = wide.tile([P, W, 4], BF16, name="y_grouped", align_bytes=64)
+            interleave("v", grouped[:], y_rows[g, h][:])
+            codes = wide.tile([P, W], U32, name="y_codes", align_bytes=64)
+            nc.vector.quantize_mx(
+                out=codes[:].bitcast(FP8X4),
+                scales=y_scales[h][:, g, :],
+                in_=grouped[:].rearrange("p j t -> p (j t)"),
+            )
+            words = out_1[g].rearrange("p m t -> p (m t)").bitcast(I32)
+            nc.sync.dma_start(out=words[:, W * h : W * (h + 1)], in_=codes[:].bitcast(I32))
+            if g == 1:
+                for q in range(4):
+                    nc.sync.dma_start(
+                        out=out_2[:, 4 * q : 4 * q + 4, W * h : W * (h + 1)].rearrange("g r c -> r g c").bitcast(I32),
+                        in_=y_scales[h][32 * q : 32 * q + 4].bitcast(I32),
+                    )
+
+        look_up_codes(0)
+        quantise_wa(0)
+        look_up_codes(1)
+        for i in range(4):
+            if i == 6:
+                quantise_wa(1)
+            project(i)
+        for i in range(16):
+            if i + 4 == 6:
+                quantise_wa(1)
+            if i + 4 < 16:
+                project(i + 4)
+            modulate(i)
+            if i == 11:
+                deal_w4()
+            if steps[i][1] == 3:
+                quantise_h(steps[i][0], steps[i][2])
+        for h in range(2):
+            for g in range(2):
+                for t in range(4):
+                    second_slice(g, t, h)
+                quantise_y(g, h)

@@ -14,12 +14,23 @@ U8 = mybir.dt.uint8
 FP8X4 = mybir.dt.float8_e4m3fn_x4
 FP4X4 = mybir.dt.float4_e2m1fn_x4
 MULT = mybir.AluOpType.mult
-ADD = mybir.AluOpType.add
 SIN = mybir.ActivationFunctionType.Sin
 COPY = mybir.ActivationFunctionType.Copy
 
 P = 128
-W = 512
+PACK = 4
+GROUP = P * PACK
+GROUPS = H // GROUP
+HALF = S // 2
+QUADRANTS = 4
+ALIGN = 64
+
+STEPS = [(0, t, half) for t in range(PACK) for half in range(2)] + [
+    (1, t, half) for half in range(2) for t in range(PACK)
+]
+LAST_OF_HALF_0 = STEPS.index((1, PACK - 1, 0))
+AHEAD = 2
+WEAVE_AFTER = {(0, 0): STEPS.index((1, 1, 0)), (0, 1): STEPS.index((1, 2, 1))}
 
 
 def tile_list_implicit_audio_sines_kernel(
@@ -28,218 +39,240 @@ def tile_list_implicit_audio_sines_kernel(
     nc = tc.nc
     with ExitStack() as ctx:
         keep = ctx.enter_context(tc.tile_pool(name="keep", bufs=1))
-        ring = ctx.enter_context(tc.tile_pool(name="ring", bufs=4))
-        wide = ctx.enter_context(tc.tile_pool(name="wide", bufs=2))
+        ring = ctx.enter_context(tc.tile_pool(name="ring", bufs=6))
+        twin = ctx.enter_context(tc.tile_pool(name="twin", bufs=2))
         psum = ctx.enter_context(tc.psum_pool(name="psum", bufs=8))
 
+        def big_tile(name):
+            return keep.tile([P, PACK, HALF], F32, name=name, tag="big", bufs=4)
+
         offsets = keep.tile([P, S // 16], U16, name="offsets")
-        tabw = keep.tile([P, T], I32, name="tabw", align_bytes=64)
-        tabs = keep.tile([P, T], U8, name="tabs", align_bytes=64)
-        wa_raw = [keep.tile([P, 4, 512], F32, name=f"wa_raw{b}", tag="big", bufs=4) for b in range(2)]
-        freq = [keep.tile([P, T], F32, name=f"freq{s}") for s in range(8)]
-        w4_raw = keep.tile([P, 2, N // 2], I32, name="w4_raw", align_bytes=64)
-        w4s_raw = keep.tile([P, 2, N], U8, name="w4s_raw", align_bytes=64)
-        gain_sb = keep.tile([P, 2, 4], F32, name="gain_sb")
-        amp_sb = keep.tile([P, 2, 4], F32, name="amp_sb")
+        table_words = keep.tile([P, T], I32, name="table_words", align_bytes=ALIGN)
+        table_scales = keep.tile([P, T], U8, name="table_scales", align_bytes=ALIGN)
+        wa_raw = [big_tile(f"wa_raw{b}") for b in range(GROUPS)]
+        freq = [keep.tile([P, T], F32, name=f"freq{s}") for s in range(GROUPS * PACK)]
+        w4_raw = keep.tile([P, GROUPS, N // 2], I32, name="w4_raw", align_bytes=ALIGN)
+        w4_raw_scales = keep.tile([P, GROUPS, N], U8, name="w4_raw_scales", align_bytes=ALIGN)
+        gain_sb = keep.tile([P, GROUPS, PACK], F32, name="gain_sb")
+        amp_sb = keep.tile([P, GROUPS, PACK], F32, name="amp_sb")
 
-        nc.vector.memset(tabs[:].bitcast(I32), 0)
-        nc.gpsimd.memset(w4s_raw[:].bitcast(I32), 0)
+        nc.vector.memset(table_scales[:].bitcast(I32), 0)
+        nc.gpsimd.memset(w4_raw_scales[:].bitcast(I32), 0)
 
-        wa_rows = wa.rearrange("(p j) c -> p j c", j=4)
-        g_rows = gT.rearrange("(b p t) c -> b t p c", b=2, t=4)
-
-        def load_freq(s):
-            nc.sync.dma_start(out=freq[s][:], in_=g_rows[s // 4, s % 4])
+        wa_rows = wa.rearrange("(p j) r -> p j r", j=PACK)
+        freq_rows = gT.rearrange("(b p t) c -> b t p c", b=GROUPS, t=PACK)
 
         def load_wa(b):
-            nc.sync.dma_start(out=wa_raw[b][:], in_=wa_rows[:, :, 512 * b : 512 * (b + 1)])
+            nc.sync.dma_start(out=wa_raw[b][:], in_=wa_rows[:, :, GROUP * b : GROUP * (b + 1)])
+
+        def load_freq(b, t):
+            nc.sync.dma_start(out=freq[PACK * b + t][:], in_=freq_rows[b, t])
 
         nc.sync.dma_start(offsets[:], offs)
         load_wa(0)
-        for q in range(4):
+        for q in range(QUADRANTS):
             nc.sync.dma_start(
-                out=tabs[32 * q : 32 * q + 4, :].bitcast(I32), in_=tab_scales[0, 4 * q : 4 * q + 4, :].bitcast(I32)
+                out=table_scales[32 * q : 32 * q + 4, :].bitcast(I32),
+                in_=tab_scales[0, 4 * q : 4 * q + 4, :].bitcast(I32),
             )
-        nc.sync.dma_start(out=tabw[:], in_=tab_words[0].rearrange("p n t -> p (n t)").bitcast(I32))
-        for q in range(4):
-            nc.gpsimd.dma_start(
-                out=w4s_raw[32 * q : 32 * q + 4].bitcast(I32),
-                in_=w4_scales[:, 4 * q : 4 * q + 4, :].rearrange("a r c -> r a c").bitcast(I32),
-            )
-        load_freq(0)
-        nc.sync.dma_start(out=gain_sb[:], in_=gain.rearrange("(b p t) -> p b t", b=2, t=4))
-        load_freq(1)
+        nc.sync.dma_start(out=table_words[:], in_=tab_words[0].rearrange("p c i -> p (c i)").bitcast(I32))
+        load_freq(0, 0)
+        nc.sync.dma_start(out=gain_sb[:], in_=gain.rearrange("(b p t) -> p b t", b=GROUPS, t=PACK))
+        load_freq(0, 1)
         load_wa(1)
-        load_freq(2)
-        load_freq(3)
-        load_freq(4)
-        load_freq(5)
-        load_freq(6)
-        load_freq(7)
-        nc.sync.dma_start(out=w4_raw[:], in_=w4_words.rearrange("a p c -> p a c").bitcast(I32))
-        nc.sync.dma_start(out=amp_sb[:], in_=amp.rearrange("(g p t) -> p g t", g=2, t=4))
+        load_freq(0, 2)
+        load_freq(0, 3)
+        nc.sync.dma_start(out=w4_raw[:], in_=w4_words.rearrange("b p c -> p b c").bitcast(I32))
+        for q in range(QUADRANTS):
+            nc.sync.dma_start(
+                out=w4_raw_scales[32 * q : 32 * q + 4].bitcast(I32),
+                in_=w4_scales[:, 4 * q : 4 * q + 4, :].rearrange("b q c -> q b c").bitcast(I32),
+            )
+        for t in range(PACK):
+            load_freq(1, t)
+        nc.sync.dma_start(out=amp_sb[:], in_=amp.rearrange("(g p t) -> p g t", g=GROUPS, t=PACK))
 
-        v_codes = [keep.tile([P, W], U32, name=f"v_codes{h}", align_bytes=64) for h in range(2)]
-        v_scales = [keep.tile([P, W], U8, name=f"v_scales{h}", align_bytes=64) for h in range(2)]
-        wa_codes = [keep.tile([P, 512], U32, name=f"wa_codes{b}", align_bytes=64) for b in range(2)]
-        wa_scales = [keep.tile([P, 512], U8, name=f"wa_scales{b}", align_bytes=64) for b in range(2)]
-        w4_codes = keep.tile([P, 2, 2 * N], U8, name="w4_codes", align_bytes=64)
-        w4_planes = keep.tile([P, 2, N], U8, name="w4_planes", align_bytes=64)
+        v_codes = [keep.tile([P, HALF], U32, name=f"v_codes{half}", align_bytes=ALIGN) for half in range(2)]
+        v_scales = [keep.tile([P, HALF], U8, name=f"v_scales{half}", align_bytes=ALIGN) for half in range(2)]
+        wa_codes = [keep.tile([P, GROUP], U32, name=f"wa_codes{b}", align_bytes=ALIGN) for b in range(GROUPS)]
+        wa_scales = [keep.tile([P, GROUP], U8, name=f"wa_scales{b}", align_bytes=ALIGN) for b in range(GROUPS)]
+        w4_codes = keep.tile([P, GROUPS, 2 * N], U8, name="w4_codes", align_bytes=ALIGN)
+        w4_dealt_scales = keep.tile([P, GROUPS, N], U8, name="w4_dealt_scales", align_bytes=ALIGN)
         h_codes = {}
         h_scales = {}
-        for b in range(2):
-            for h in range(2):
-                h_codes[b, h] = keep.tile([P, W], U32, name=f"h_codes{b}{h}", align_bytes=64)
-                h_scales[b, h] = keep.tile([P, W], U8, name=f"h_scales{b}{h}", align_bytes=64)
-        y_scales = [keep.tile([P, 2, W], U8, name=f"y_scales{h}", align_bytes=64) for h in range(2)]
+        for b in range(GROUPS):
+            for half in range(2):
+                h_codes[b, half] = keep.tile([P, HALF], U32, name=f"h_codes{b}{half}", align_bytes=ALIGN)
+                h_scales[b, half] = keep.tile([P, HALF], U8, name=f"h_scales{b}{half}", align_bytes=ALIGN)
+        y_scales = keep.tile([P, GROUPS, S], U8, name="y_scales", align_bytes=ALIGN)
 
-        def half_list(h):
-            return offsets[:, h * (W // 16) : (h + 1) * (W // 16)]
+        def half_list(half):
+            return offsets[:, half * (HALF // 16) : (half + 1) * (HALF // 16)]
 
-        def look_up_codes(h):
-            nc.vector.tensor_copy(out=v_codes[h][:], in_=tabw[:].bitcast(U32).indirect(half_list(h)))
-            nc.vector.tensor_copy(out=v_scales[h][:], in_=tabs[:].indirect(half_list(h)))
+        def look_up_codes(half):
+            nc.vector.tensor_copy(out=v_codes[half][:], in_=table_words[:].bitcast(U32).indirect(half_list(half)))
+            nc.vector.tensor_copy(out=v_scales[half][:], in_=table_scales[:].indirect(half_list(half)))
 
-        def quantise_wa(b):
-            grouped = wide.tile([P, 4, P, 4], BF16, name="wa_grouped", align_bytes=64)
-            (nc.vector.tensor_copy if ("v" if b else "s") == "v" else nc.scalar.copy)(
-                out=grouped[:].rearrange("p t m j -> p m j t"),
-                in_=wa_raw[b][:].rearrange("p j (m t) -> p m j t", t=4),
+        def weave_wa(b, copy):
+            woven = twin.tile([P, PACK, P, PACK], BF16, name="wa_woven", tag="woven", align_bytes=ALIGN)
+            copy(
+                out=woven[:].rearrange("p t m j -> p m j t"),
+                in_=wa_raw[b][:].rearrange("p j (m t) -> p m j t", t=PACK),
             )
-            nc.vector.quantize_mx(
-                out=wa_codes[b][:].bitcast(FP8X4),
-                scales=wa_scales[b][:],
-                in_=grouped[:].rearrange("p t m j -> p (t m j)"),
-            )
+            return woven[:].rearrange("p t m j -> p (t m j)")
+
+        def quantise(woven, codes, scales):
+            nc.vector.quantize_mx(out=codes.bitcast(FP8X4), scales=scales, in_=woven)
 
         def deal_w4():
+            dealt, natural = "p b (g t m) -> p (b g) t m", "p b (g m t) -> p (b g) t m"
             nc.vector.tensor_copy(
-                out=w4_codes[:].bitcast(U16).rearrange("p a (g t m) -> p (a g) t m", g=2, t=4),
-                in_=w4_raw[:].bitcast(U16).rearrange("p a (g m t) -> p (a g) t m", g=2, t=4),
+                out=w4_codes[:].bitcast(U16).rearrange(dealt, g=GROUPS, t=PACK),
+                in_=w4_raw[:].bitcast(U16).rearrange(natural, g=GROUPS, t=PACK),
             )
             nc.vector.tensor_copy(
-                out=w4_planes[:].rearrange("p a (g t m) -> p (a g) t m", g=2, t=4),
-                in_=w4s_raw[:].rearrange("p a (g m t) -> p (a g) t m", g=2, t=4),
+                out=w4_dealt_scales[:].rearrange(dealt, g=GROUPS, t=PACK),
+                in_=w4_raw_scales[:].rearrange(natural, g=GROUPS, t=PACK),
             )
 
-        def interleave(eng, dst, src):
-            d = dst.rearrange("p (c i) t -> p c t i", i=4)
-            s = src.rearrange("p t (c i) -> p c t i", i=4)
-            if eng == "v":
-                nc.vector.tensor_copy(out=d, in_=s)
-            elif eng == "s":
-                nc.scalar.copy(out=d, in_=s)
-            else:
-                nc.gpsimd.tensor_scalar(out=d, in0=s, scalar1=1.0, scalar2=0.0, op0=MULT, op1=ADD)
+        def weave(woven, rows):
+            nc.vector.tensor_copy(
+                out=woven[:].rearrange("p (c i) t -> p c t i", i=4),
+                in_=rows[:].rearrange("p t (c i) -> p c t i", i=4),
+            )
+            return woven[:].rearrange("p j t -> p (j t)")
 
-        def scale_rows(eng, dst, src, col):
-            if eng == "v":
-                nc.vector.tensor_scalar(out=dst, in0=src, scalar1=col, scalar2=None, op0=MULT)
-            elif eng == "s":
-                nc.scalar.activation(out=dst, in_=src, func=COPY, scale=col)
+        def scale_rows(on_scalar, out, sine, factor):
+            if on_scalar:
+                nc.scalar.activation(out=out, in_=sine, func=COPY, scale=factor)
             else:
-                nc.gpsimd.tensor_scalar(out=dst, in0=src, scalar1=col, scalar2=0.0, op0=MULT, op1=ADD)
+                nc.vector.tensor_scalar(out=out, in0=sine, scalar1=factor, scalar2=None, op0=MULT)
 
+        taken = set(WEAVE_AFTER.values()) | {LAST_OF_HALF_0}
+        pair_tag = {LAST_OF_HALF_0 + 1: f"slot{LAST_OF_HALF_0}", LAST_OF_HALF_0 + 3: "h_rows10"}
+        projections = {}
+        phases = {}
         h_rows = {}
 
-        slots = [keep.tile([P, W], F32, name=f"slot{i}") for i in range(12)]
-        steps = [(0, t, h) for t in range(4) for h in range(2)] + [(1, t, h) for h in range(2) for t in range(4)]
-
         def project(i):
-            b, t, h = steps[i]
-            acc = psum.tile([P, W], F32, name="acc")
+            b, t, half = STEPS[i]
+            acc = psum.tile([P, HALF], F32, name="acc")
             cols = slice(P * t, P * (t + 1))
             nc.tensor.matmul_mx(
                 out=acc[:],
                 lhsT=wa_codes[b][:, cols].bitcast(FP8X4),
                 lhsT_scale=wa_scales[b][:, cols],
-                rhs=v_codes[h][:].bitcast(FP8X4),
-                rhs_scale=v_scales[h][:],
+                rhs=v_codes[half][:].bitcast(FP8X4),
+                rhs_scale=v_scales[half][:],
                 start=True,
                 stop=True,
             )
-            nc.scalar.copy(out=slots[(i + 2) % 12][:], in_=acc[:])
+            projections[i] = keep.tile([P, HALF], F32, name=f"projection{i}", tag=f"slot{i}", align_bytes=ALIGN)
+            nc.scalar.copy(out=projections[i][:], in_=acc[:])
+
+        def place_phase(i):
+            if i in pair_tag:
+                pair = keep.tile([P, 2, HALF], F32, name=f"phase_pair{i}", tag=pair_tag[i], align_bytes=ALIGN)
+                phases[i], phases[i + 1] = pair[:, 0, :], pair[:, 1, :]
+            elif i not in phases:
+                inherits = i >= AHEAD and i - AHEAD not in taken
+                tag = f"slot{i - AHEAD}" if inherits else f"phase{i}"
+                phases[i] = keep.tile([P, HALF], F32, name=f"phase{i}", tag=tag, align_bytes=ALIGN)[:]
+            return phases[i]
 
         def modulate(i):
-            b, t, h = steps[i]
+            b, t, half = STEPS[i]
             if t == 0:
-                h_rows[b, h] = wide.tile([P, 4, W], BF16, name="h_rows", bufs=2)
-            proj = slots[(i + 2) % 12]
-            phase = slots[(i + 0) % 12]
-            nc.vector.tensor_tensor(out=phase[:], in0=freq[4 * b + t][:].indirect(half_list(h)), in1=proj[:], op=MULT)
-            sine = ring.tile([P, W], F32, name="sine")
-            nc.scalar.activation(out=sine[:], in_=phase[:], func=SIN)
-            scale_rows("v" if i >= 14 else "s", h_rows[b, h][:, t, :], sine[:], gain_sb[:, b, t : t + 1])
+                h_rows[b, half] = keep.tile([P, PACK, HALF], BF16, name=f"h_rows{b}{half}", align_bytes=ALIGN)
+            phase = place_phase(i)
+            window = freq[PACK * b + t][:].indirect(half_list(half))
+            nc.vector.tensor_tensor(out=phase, in0=window, in1=projections[i][:], op=MULT)
+            if i - LAST_OF_HALF_0 in (0, 1):
+                sine = keep.tile([P, HALF], F32, name=f"sine{i}", tag="held_sine")
+            else:
+                sine = ring.tile([P, HALF], F32, name="sine")
+            nc.scalar.activation(out=sine[:], in_=phase, func=SIN)
+            scale_rows(i <= LAST_OF_HALF_0, h_rows[b, half][:, t, :], sine[:], gain_sb[:, b, t : t + 1])
 
-        def quantise_h(b, h):
-            grouped = wide.tile([P, W, 4], BF16, name="h_grouped", align_bytes=64)
-            interleave("v", grouped[:], h_rows[b, h][:])
-            nc.vector.quantize_mx(
-                out=h_codes[b, h][:].bitcast(FP8X4),
-                scales=h_scales[b, h][:],
-                in_=grouped[:].rearrange("p j t -> p (j t)"),
-            )
+        def quantise_h(b, half):
+            tag = f"slot{WEAVE_AFTER[b, half]}" if (b, half) in WEAVE_AFTER else f"h_woven{b}{half}"
+            woven = keep.tile([P, HALF, PACK], BF16, name=f"h_woven{b}{half}", tag=tag, align_bytes=ALIGN)
+            quantise(weave(woven, h_rows[b, half]), h_codes[b, half][:], h_scales[b, half][:])
 
         y_rows = {}
-        y_out = out_0.rearrange("(g p t) j -> g p t j", g=2, t=4)
+        y_codes = {}
+        y_out = out_0.rearrange("(g p t) j -> g p t j", g=GROUPS, t=PACK)
 
-        def second_slice(g, t, h):
+        def output_slice(g, t, half):
             if t == 0:
-                y_rows[g, h] = keep.tile([P, 4, W], F32, name=f"y_rows{g}{h}", tag="big", bufs=4)
-            acc = psum.tile([P, W], F32, name="acc")
-            c0 = 512 * g + P * t
-            for b in range(2):
+                y_rows[g, half] = big_tile(f"y_rows{g}{half}")
+            acc = psum.tile([P, HALF], F32, name="acc")
+            first = GROUP * g + P * t
+            for b in range(GROUPS):
                 nc.tensor.matmul_mx(
                     out=acc[:],
-                    lhsT=w4_codes[:, b, 2 * c0 : 2 * (c0 + P)].bitcast(FP4X4),
-                    lhsT_scale=w4_planes[:, b, c0 : c0 + P],
-                    rhs=h_codes[b, h][:].bitcast(FP8X4),
-                    rhs_scale=h_scales[b, h][:],
+                    lhsT=w4_codes[:, b, 2 * first : 2 * (first + P)].bitcast(FP4X4),
+                    lhsT_scale=w4_dealt_scales[:, b, first : first + P],
+                    rhs=h_codes[b, half][:].bitcast(FP8X4),
+                    rhs_scale=h_scales[b, half][:],
                     start=(b == 0),
-                    stop=(b == 1),
+                    stop=(b == GROUPS - 1),
                 )
-            sine = ring.tile([P, W], F32, name="sine2")
+            sine = ring.tile([P, HALF], F32, name="sine")
             nc.scalar.activation(out=sine[:], in_=acc[:], func=SIN)
-            scale_rows("s" if t == 0 else "v", y_rows[g, h][:, t, :], sine[:], amp_sb[:, g, t : t + 1])
-            nc.sync.dma_start(out=y_out[g, :, t, W * h : W * (h + 1)], in_=y_rows[g, h][:, t, :])
+            on_scalar = t == PACK - 1 or ((g, half) == (0, 0) and t < 2)
+            scale_rows(on_scalar, y_rows[g, half][:, t, :], sine[:], amp_sb[:, g, t : t + 1])
+            if t % 2:
+                nc.sync.dma_start(
+                    out=y_out[g, :, t - 1 : t + 1, HALF * half : HALF * (half + 1)],
+                    in_=y_rows[g, half][:, t - 1 : t + 1, :],
+                )
 
-        def quantise_y(g, h):
-            grouped = wide.tile([P, W, 4], BF16, name="y_grouped", align_bytes=64)
-            interleave("v", grouped[:], y_rows[g, h][:])
-            codes = wide.tile([P, W], U32, name="y_codes", align_bytes=64)
-            nc.vector.quantize_mx(
-                out=codes[:].bitcast(FP8X4),
-                scales=y_scales[h][:, g, :],
-                in_=grouped[:].rearrange("p j t -> p (j t)"),
-            )
+        def quantise_y(g, half):
+            y_codes[g, half] = twin.tile([P, HALF], U32, name="y_codes", align_bytes=ALIGN, bufs=3)
+            woven = twin.tile([P, HALF, PACK], BF16, name="y_woven", tag="woven", align_bytes=ALIGN)
+            scales = y_scales[:, g, HALF * half : HALF * (half + 1)]
+            quantise(weave(woven, y_rows[g, half]), y_codes[g, half][:], scales)
+
+        def store_codes(g, half):
             words = out_1[g].rearrange("p m t -> p (m t)").bitcast(I32)
-            nc.sync.dma_start(out=words[:, W * h : W * (h + 1)], in_=codes[:].bitcast(I32))
-            if g == 1:
-                for q in range(4):
-                    nc.sync.dma_start(
-                        out=out_2[:, 4 * q : 4 * q + 4, W * h : W * (h + 1)].rearrange("g r c -> r g c").bitcast(I32),
-                        in_=y_scales[h][32 * q : 32 * q + 4].bitcast(I32),
-                    )
+            nc.sync.dma_start(out=words[:, HALF * half : HALF * (half + 1)], in_=y_codes[g, half][:].bitcast(I32))
 
         look_up_codes(0)
-        quantise_wa(0)
+        quantise(weave_wa(0, nc.scalar.copy), wa_codes[0][:], wa_scales[0][:])
         look_up_codes(1)
-        for i in range(4):
-            if i == 6:
-                quantise_wa(1)
+        for i in range(AHEAD):
             project(i)
-        for i in range(16):
-            if i + 4 == 6:
-                quantise_wa(1)
-            if i + 4 < 16:
-                project(i + 4)
+        for i, (b, t, half) in enumerate(STEPS):
+            if (b, t, half) == (0, 1, 1):
+                quantise(weave_wa(1, nc.vector.tensor_copy), wa_codes[1][:], wa_scales[1][:])
+            if i + AHEAD < len(STEPS):
+                project(i + AHEAD)
             modulate(i)
-            if i == 11:
+            if (b, t, half) == (0, PACK - 1, 1):
                 deal_w4()
-            if steps[i][1] == 3:
-                quantise_h(steps[i][0], steps[i][2])
-        for h in range(2):
-            for g in range(2):
-                for t in range(4):
-                    second_slice(g, t, h)
-                quantise_y(g, h)
+            if i == LAST_OF_HALF_0:
+                quantise_h(1, 0)
+            for key, after in WEAVE_AFTER.items():
+                if i == after:
+                    quantise_h(*key)
+            if i > LAST_OF_HALF_0:
+                output_slice(0, t, 0)
+        quantise_h(1, 1)
+
+        quarters = [(g, half) for half in range(2) for g in range(GROUPS)]
+        for n in range(1, len(quarters)):
+            g, half = quarters[n]
+            for t in range(PACK):
+                output_slice(g, t, half)
+            if n >= 2:
+                store_codes(*quarters[n - 2])
+            quantise_y(*quarters[n - 1])
+        quantise_y(*quarters[-1])
+        store_codes(*quarters[-2])
+        store_codes(*quarters[-1])
+        for q in range(QUADRANTS):
+            nc.sync.dma_start(
+                out=out_2[:, 4 * q : 4 * q + 4, :].rearrange("g q c -> q g c").bitcast(I32),
+                in_=y_scales[32 * q : 32 * q + 4].bitcast(I32),
+            )

@@ -28,9 +28,9 @@ ALIGN = 64
 STEPS = [(0, t, half) for t in range(PACK) for half in range(2)] + [
     (1, t, half) for half in range(2) for t in range(PACK)
 ]
-LAST_OF_HALF_0 = STEPS.index((1, PACK - 1, 0))
+PIVOT = STEPS.index((1, PACK - 1, 0))
 AHEAD = 2
-WEAVE_AFTER = {(0, 0): STEPS.index((1, 1, 0)), (0, 1): STEPS.index((1, 2, 1))}
+WEAVE_00_AFTER = STEPS.index((1, 1, 0))
 
 
 def tile_list_implicit_audio_sines_kernel(
@@ -52,7 +52,7 @@ def tile_list_implicit_audio_sines_kernel(
         wa_raw = [big_tile(f"wa_raw{b}") for b in range(GROUPS)]
         freq = [keep.tile([P, T], F32, name=f"freq{s}") for s in range(GROUPS * PACK)]
         w4_raw = keep.tile([P, GROUPS, N // 2], I32, name="w4_raw", align_bytes=ALIGN)
-        w4_raw_scales = keep.tile([P, GROUPS, N], U8, name="w4_raw_scales", align_bytes=ALIGN)
+        w4_raw_scales = keep.tile([P, N], U8, name="w4_raw_scales", align_bytes=ALIGN)
         gain_sb = keep.tile([P, GROUPS, PACK], F32, name="gain_sb")
         amp_sb = keep.tile([P, GROUPS, PACK], F32, name="amp_sb")
 
@@ -85,8 +85,8 @@ def tile_list_implicit_audio_sines_kernel(
         nc.sync.dma_start(out=w4_raw[:], in_=w4_words.rearrange("b p c -> p b c").bitcast(I32))
         for q in range(QUADRANTS):
             nc.sync.dma_start(
-                out=w4_raw_scales[32 * q : 32 * q + 4].bitcast(I32),
-                in_=w4_scales[:, 4 * q : 4 * q + 4, :].rearrange("b q c -> q b c").bitcast(I32),
+                out=w4_raw_scales[32 * q : 32 * q + 8, :].bitcast(I32),
+                in_=w4_scales[:, 4 * q : 4 * q + 4, :].bitcast(I32),
             )
         for t in range(PACK):
             load_freq(1, t)
@@ -97,7 +97,8 @@ def tile_list_implicit_audio_sines_kernel(
         wa_codes = [keep.tile([P, GROUP], U32, name=f"wa_codes{b}", align_bytes=ALIGN) for b in range(GROUPS)]
         wa_scales = [keep.tile([P, GROUP], U8, name=f"wa_scales{b}", align_bytes=ALIGN) for b in range(GROUPS)]
         w4_codes = keep.tile([P, GROUPS, 2 * N], U8, name="w4_codes", align_bytes=ALIGN)
-        w4_dealt_scales = keep.tile([P, GROUPS, N], U8, name="w4_dealt_scales", align_bytes=ALIGN)
+        w4_dealt_scales = [keep.tile([P, N], U8, name=f"w4_dealt_scales{b}", align_bytes=ALIGN) for b in range(GROUPS)]
+        nc.gpsimd.memset(w4_dealt_scales[1][:].bitcast(I32), 0)
         h_codes = {}
         h_scales = {}
         for b in range(GROUPS):
@@ -131,9 +132,14 @@ def tile_list_implicit_audio_sines_kernel(
                 in_=w4_raw[:].bitcast(U16).rearrange(natural, g=GROUPS, t=PACK),
             )
             nc.vector.tensor_copy(
-                out=w4_dealt_scales[:].rearrange(dealt, g=GROUPS, t=PACK),
-                in_=w4_raw_scales[:].rearrange(natural, g=GROUPS, t=PACK),
+                out=w4_dealt_scales[0][:].rearrange("p (g t m) -> p g t m", g=GROUPS, t=PACK),
+                in_=w4_raw_scales[:].rearrange("p (g m t) -> p g t m", g=GROUPS, t=PACK),
             )
+            for q in range(QUADRANTS):
+                nc.sync.dma_start(
+                    out=w4_dealt_scales[1][32 * q : 32 * q + 4, :].bitcast(I32),
+                    in_=w4_dealt_scales[0][32 * q + 4 : 32 * q + 8, :].bitcast(I32),
+                )
 
         def weave(woven, rows):
             nc.vector.tensor_copy(
@@ -148,13 +154,13 @@ def tile_list_implicit_audio_sines_kernel(
             else:
                 nc.vector.tensor_scalar(out=out, in0=sine, scalar1=factor, scalar2=None, op0=MULT)
 
-        taken = set(WEAVE_AFTER.values()) | {LAST_OF_HALF_0}
-        pair_tag = {LAST_OF_HALF_0 + 1: f"slot{LAST_OF_HALF_0}", LAST_OF_HALF_0 + 3: "h_rows10"}
         projections = {}
-        phases = {}
         h_rows = {}
 
-        def project(i):
+        def rows_tile(name, tag, rows=1):
+            return keep.tile([P, HALF] if rows == 1 else [P, rows, HALF], F32, name=name, tag=tag, align_bytes=ALIGN)
+
+        def project(i, tag):
             b, t, half = STEPS[i]
             acc = psum.tile([P, HALF], F32, name="acc")
             cols = slice(P * t, P * (t + 1))
@@ -167,61 +173,47 @@ def tile_list_implicit_audio_sines_kernel(
                 start=True,
                 stop=True,
             )
-            projections[i] = keep.tile([P, HALF], F32, name=f"projection{i}", tag=f"slot{i}", align_bytes=ALIGN)
+            projections[i] = rows_tile(f"projection{i}", tag)
             nc.scalar.copy(out=projections[i][:], in_=acc[:])
 
-        def place_phase(i):
-            if i in pair_tag:
-                pair = keep.tile([P, 2, HALF], F32, name=f"phase_pair{i}", tag=pair_tag[i], align_bytes=ALIGN)
-                phases[i], phases[i + 1] = pair[:, 0, :], pair[:, 1, :]
-            elif i not in phases:
-                inherits = i >= AHEAD and i - AHEAD not in taken
-                tag = f"slot{i - AHEAD}" if inherits else f"phase{i}"
-                phases[i] = keep.tile([P, HALF], F32, name=f"phase{i}", tag=tag, align_bytes=ALIGN)[:]
-            return phases[i]
-
-        def modulate(i):
+        def modulate(i, phase, sine):
             b, t, half = STEPS[i]
             if t == 0:
                 h_rows[b, half] = keep.tile([P, PACK, HALF], BF16, name=f"h_rows{b}{half}", align_bytes=ALIGN)
-            phase = place_phase(i)
             window = freq[PACK * b + t][:].indirect(half_list(half))
             nc.vector.tensor_tensor(out=phase, in0=window, in1=projections[i][:], op=MULT)
-            if i - LAST_OF_HALF_0 in (0, 1):
-                sine = keep.tile([P, HALF], F32, name=f"sine{i}", tag="held_sine")
-            else:
-                sine = ring.tile([P, HALF], F32, name="sine")
-            nc.scalar.activation(out=sine[:], in_=phase, func=SIN)
-            scale_rows(i <= LAST_OF_HALF_0, h_rows[b, half][:, t, :], sine[:], gain_sb[:, b, t : t + 1])
+            nc.scalar.activation(out=sine, in_=phase, func=SIN)
+            scale_rows(i < len(STEPS) - 3, h_rows[b, half][:, t, :], sine, gain_sb[:, b, t : t + 1])
 
-        def quantise_h(b, half):
-            tag = f"slot{WEAVE_AFTER[b, half]}" if (b, half) in WEAVE_AFTER else f"h_woven{b}{half}"
+        def quantise_h(b, half, tag):
             woven = keep.tile([P, HALF, PACK], BF16, name=f"h_woven{b}{half}", tag=tag, align_bytes=ALIGN)
             quantise(weave(woven, h_rows[b, half]), h_codes[b, half][:], h_scales[b, half][:])
+
+        def ring_sine():
+            return ring.tile([P, HALF], F32, name="sine")[:]
 
         y_rows = {}
         y_codes = {}
         y_out = out_0.rearrange("(g p t) j -> g p t j", g=GROUPS, t=PACK)
 
-        def output_slice(g, t, half):
+        def output_slice(g, t, half, sine):
             if t == 0:
                 y_rows[g, half] = big_tile(f"y_rows{g}{half}")
             acc = psum.tile([P, HALF], F32, name="acc")
-            first = GROUP * g + P * t
+            col = GROUP * g + P * t
             for b in range(GROUPS):
                 nc.tensor.matmul_mx(
                     out=acc[:],
-                    lhsT=w4_codes[:, b, 2 * first : 2 * (first + P)].bitcast(FP4X4),
-                    lhsT_scale=w4_dealt_scales[:, b, first : first + P],
+                    lhsT=w4_codes[:, b, 2 * col : 2 * (col + P)].bitcast(FP4X4),
+                    lhsT_scale=w4_dealt_scales[b][:, col : col + P],
                     rhs=h_codes[b, half][:].bitcast(FP8X4),
                     rhs_scale=h_scales[b, half][:],
                     start=(b == 0),
                     stop=(b == GROUPS - 1),
                 )
-            sine = ring.tile([P, HALF], F32, name="sine")
-            nc.scalar.activation(out=sine[:], in_=acc[:], func=SIN)
+            nc.scalar.activation(out=sine, in_=acc[:], func=SIN)
             on_scalar = t == PACK - 1 or ((g, half) == (0, 0) and t < 2)
-            scale_rows(on_scalar, y_rows[g, half][:, t, :], sine[:], amp_sb[:, g, t : t + 1])
+            scale_rows(on_scalar, y_rows[g, half][:, t, :], sine, amp_sb[:, g, t : t + 1])
             if t % 2:
                 nc.sync.dma_start(
                     out=y_out[g, :, t - 1 : t + 1, HALF * half : HALF * (half + 1)],
@@ -242,29 +234,42 @@ def tile_list_implicit_audio_sines_kernel(
         quantise(weave_wa(0, nc.scalar.copy), wa_codes[0][:], wa_scales[0][:])
         look_up_codes(1)
         for i in range(AHEAD):
-            project(i)
-        for i, (b, t, half) in enumerate(STEPS):
-            if (b, t, half) == (0, 1, 1):
+            project(i, f"slot{i}")
+        for i in range(PIVOT + 1):
+            if STEPS[i] == (0, 1, 1):
                 quantise(weave_wa(1, nc.vector.tensor_copy), wa_codes[1][:], wa_scales[1][:])
-            if i + AHEAD < len(STEPS):
-                project(i + AHEAD)
-            modulate(i)
-            if (b, t, half) == (0, PACK - 1, 1):
+            project(i + AHEAD, f"slot{i + AHEAD}")
+            inherits = i >= AHEAD and i - AHEAD != WEAVE_00_AFTER
+            phase = rows_tile(f"phase{i}", f"slot{i - AHEAD}" if inherits else f"phase{i}")
+            modulate(i, phase[:], rows_tile("pivot_sine", "pivot_sine")[:] if i == PIVOT else ring_sine())
+            if STEPS[i] == (0, PACK - 1, 1):
                 deal_w4()
-            if i == LAST_OF_HALF_0:
-                quantise_h(1, 0)
-            for key, after in WEAVE_AFTER.items():
-                if i == after:
-                    quantise_h(*key)
-            if i > LAST_OF_HALF_0:
-                output_slice(0, t, 0)
-        quantise_h(1, 1)
+            if i == WEAVE_00_AFTER:
+                quantise_h(0, 0, f"slot{i}")
+        quantise_h(1, 0, "h_woven10")
+
+        first, second, third, fourth = range(PIVOT + 1, len(STEPS))
+        project(third, f"phase{PIVOT}")
+        early_phases = rows_tile("early_phases", f"slot{PIVOT}", rows=2)
+        early_sines = rows_tile("early_sines", "pivot_sine", rows=2)
+        modulate(first, early_phases[:, 0, :], early_sines[:, 0, :])
+        modulate(second, early_phases[:, 1, :], early_sines[:, 1, :])
+        project(fourth, f"slot{PIVOT}")
+        output_slice(0, 0, 0, ring_sine())
+        output_slice(0, 1, 0, rows_tile("slice_1_sine", "last_sine")[:])
+        late_phases = rows_tile("late_phases", "h_rows10", rows=2)
+        modulate(third, late_phases[:, 0, :], ring_sine())
+        quantise_h(0, 1, f"phase{PIVOT}")
+        output_slice(0, 2, 0, ring_sine())
+        modulate(fourth, late_phases[:, 1, :], rows_tile("last_sine", "last_sine")[:])
+        output_slice(0, 3, 0, ring_sine())
+        quantise_h(1, 1, "h_woven11")
 
         quarters = [(g, half) for half in range(2) for g in range(GROUPS)]
         for n in range(1, len(quarters)):
             g, half = quarters[n]
             for t in range(PACK):
-                output_slice(g, t, half)
+                output_slice(g, t, half, ring_sine())
             if n >= 2:
                 store_codes(*quarters[n - 2])
             quantise_y(*quarters[n - 1])

from contextlib import ExitStack

import concourse.mybir as mybir

K, T, S, H, N = 512, 2048, 1024, 1024, 1024
FLOPS = 2 * K * H * S + 2 * H * N * S

F32 = mybir.dt.float32
BF16 = mybir.dt.bfloat16
I32 = mybir.dt.int32
U32 = mybir.dt.uint32
U16 = mybir.dt.uint16
U8 = mybir.dt.uint8
FP8X4 = mybir.dt.float8_e4m3fn_x4
FP4X4 = mybir.dt.float4_e2m1fn_x4
MULT = mybir.AluOpType.mult
SIN = mybir.ActivationFunctionType.Sin
COPY = mybir.ActivationFunctionType.Copy

P = 128
PACK = 4
GROUP = P * PACK
GROUPS = H // GROUP
HALF = S // 2
QUADRANTS = 4
ALIGN = 64

STEPS = [(0, t, half) for t in range(PACK) for half in range(2)] + [
    (1, t, half) for half in range(2) for t in range(PACK)
]
PIVOT = STEPS.index((1, PACK - 1, 0))
AHEAD = 2
WEAVE_00_AFTER = STEPS.index((1, 1, 0))


def tile_list_implicit_audio_sines_kernel(
    tc, tab_words, tab_scales, offs, wa, gT, gain, w4_words, w4_scales, amp, out_0, out_1, out_2
):
    nc = tc.nc
    with ExitStack() as ctx:
        keep = ctx.enter_context(tc.tile_pool(name="keep", bufs=1))
        ring = ctx.enter_context(tc.tile_pool(name="ring", bufs=6))
        twin = ctx.enter_context(tc.tile_pool(name="twin", bufs=2))
        psum = ctx.enter_context(tc.psum_pool(name="psum", bufs=8))

        def big_tile(name):
            return keep.tile([P, PACK, HALF], F32, name=name, tag="big", bufs=4)

        offsets = keep.tile([P, S // 16], U16, name="offsets")
        table_words = keep.tile([P, T], I32, name="table_words", align_bytes=ALIGN)
        table_scales = keep.tile([P, T], U8, name="table_scales", align_bytes=ALIGN)
        wa_raw = [big_tile(f"wa_raw{b}") for b in range(GROUPS)]
        freq = [keep.tile([P, T], F32, name=f"freq{s}") for s in range(GROUPS * PACK)]
        w4_raw = keep.tile([P, GROUPS, N // 2], I32, name="w4_raw", align_bytes=ALIGN)
        w4_raw_scales = keep.tile([P, N], U8, name="w4_raw_scales", align_bytes=ALIGN)
        gain_sb = keep.tile([P, GROUPS, PACK], F32, name="gain_sb")
        amp_sb = keep.tile([P, GROUPS, PACK], F32, name="amp_sb")

        nc.vector.memset(table_scales[:].bitcast(I32), 0)
        nc.gpsimd.memset(w4_raw_scales[:].bitcast(I32), 0)

        wa_rows = wa.rearrange("(p j) r -> p j r", j=PACK)
        freq_rows = gT.rearrange("(b p t) c -> b t p c", b=GROUPS, t=PACK)

        def load_wa(b):
            nc.sync.dma_start(out=wa_raw[b][:], in_=wa_rows[:, :, GROUP * b : GROUP * (b + 1)])

        def load_freq(b, t):
            nc.sync.dma_start(out=freq[PACK * b + t][:], in_=freq_rows[b, t])

        nc.sync.dma_start(offsets[:], offs)
        load_wa(0)
        for q in range(QUADRANTS):
            nc.sync.dma_start(
                out=table_scales[32 * q : 32 * q + 4, :].bitcast(I32),
                in_=tab_scales[0, 4 * q : 4 * q + 4, :].bitcast(I32),
            )
        nc.sync.dma_start(out=table_words[:], in_=tab_words[0].rearrange("p c i -> p (c i)").bitcast(I32))
        load_freq(0, 0)
        nc.sync.dma_start(out=gain_sb[:], in_=gain.rearrange("(b p t) -> p b t", b=GROUPS, t=PACK))
        load_freq(0, 1)
        load_wa(1)
        load_freq(0, 2)
        load_freq(0, 3)
        nc.sync.dma_start(out=w4_raw[:], in_=w4_words.rearrange("b p c -> p b c").bitcast(I32))
        for q in range(QUADRANTS):
            nc.sync.dma_start(
                out=w4_raw_scales[32 * q : 32 * q + 8, :].bitcast(I32),
                in_=w4_scales[:, 4 * q : 4 * q + 4, :].bitcast(I32),
            )
        for t in range(PACK):
            load_freq(1, t)
        nc.sync.dma_start(out=amp_sb[:], in_=amp.rearrange("(g p t) -> p g t", g=GROUPS, t=PACK))

        v_codes = [keep.tile([P, HALF], U32, name=f"v_codes{half}", align_bytes=ALIGN) for half in range(2)]
        v_scales = [keep.tile([P, HALF], U8, name=f"v_scales{half}", align_bytes=ALIGN) for half in range(2)]
        wa_codes = [keep.tile([P, GROUP], U32, name=f"wa_codes{b}", align_bytes=ALIGN) for b in range(GROUPS)]
        wa_scales = [keep.tile([P, GROUP], U8, name=f"wa_scales{b}", align_bytes=ALIGN) for b in range(GROUPS)]
        w4_codes = keep.tile([P, GROUPS, 2 * N], U8, name="w4_codes", align_bytes=ALIGN)
        w4_dealt_scales = [keep.tile([P, N], U8, name=f"w4_dealt_scales{b}", align_bytes=ALIGN) for b in range(GROUPS)]
        nc.gpsimd.memset(w4_dealt_scales[1][:].bitcast(I32), 0)
        h_codes = {}
        h_scales = {}
        for b in range(GROUPS):
            for half in range(2):
                h_codes[b, half] = keep.tile([P, HALF], U32, name=f"h_codes{b}{half}", align_bytes=ALIGN)
                h_scales[b, half] = keep.tile([P, HALF], U8, name=f"h_scales{b}{half}", align_bytes=ALIGN)
        y_scales = keep.tile([P, GROUPS, S], U8, name="y_scales", align_bytes=ALIGN)

        def half_list(half):
            return offsets[:, half * (HALF // 16) : (half + 1) * (HALF // 16)]

        def look_up_codes(half):
            nc.vector.tensor_copy(out=v_codes[half][:], in_=table_words[:].bitcast(U32).indirect(half_list(half)))
            nc.vector.tensor_copy(out=v_scales[half][:], in_=table_scales[:].indirect(half_list(half)))

        def weave_wa(b, copy):
            woven = twin.tile([P, PACK, P, PACK], BF16, name="wa_woven", tag="woven", align_bytes=ALIGN)
            copy(
                out=woven[:].rearrange("p t m j -> p m j t"),
                in_=wa_raw[b][:].rearrange("p j (m t) -> p m j t", t=PACK),
            )
            return woven[:].rearrange("p t m j -> p (t m j)")

        def quantise(woven, codes, scales):
            nc.vector.quantize_mx(out=codes.bitcast(FP8X4), scales=scales, in_=woven)

        def deal_w4():
            dealt, natural = "p b (g t m) -> p (b g) t m", "p b (g m t) -> p (b g) t m"
            nc.vector.tensor_copy(
                out=w4_codes[:].bitcast(U16).rearrange(dealt, g=GROUPS, t=PACK),
                in_=w4_raw[:].bitcast(U16).rearrange(natural, g=GROUPS, t=PACK),
            )
            nc.vector.tensor_copy(
                out=w4_dealt_scales[0][:].rearrange("p (g t m) -> p g t m", g=GROUPS, t=PACK),
                in_=w4_raw_scales[:].rearrange("p (g m t) -> p g t m", g=GROUPS, t=PACK),
            )
            for q in range(QUADRANTS):
                nc.sync.dma_start(
                    out=w4_dealt_scales[1][32 * q : 32 * q + 4, :].bitcast(I32),
                    in_=w4_dealt_scales[0][32 * q + 4 : 32 * q + 8, :].bitcast(I32),
                )

        def weave(woven, rows):
            nc.vector.tensor_copy(
                out=woven[:].rearrange("p (c i) t -> p c t i", i=4),
                in_=rows[:].rearrange("p t (c i) -> p c t i", i=4),
            )
            return woven[:].rearrange("p j t -> p (j t)")

        def scale_rows(on_scalar, out, sine, factor):
            if on_scalar:
                nc.scalar.activation(out=out, in_=sine, func=COPY, scale=factor)
            else:
                nc.vector.tensor_scalar(out=out, in0=sine, scalar1=factor, scalar2=None, op0=MULT)

        projections = {}
        h_rows = {}

        def rows_tile(name, tag, rows=1):
            return keep.tile([P, HALF] if rows == 1 else [P, rows, HALF], F32, name=name, tag=tag, align_bytes=ALIGN)

        def project(i, tag):
            b, t, half = STEPS[i]
            acc = psum.tile([P, HALF], F32, name="acc")
            cols = slice(P * t, P * (t + 1))
            nc.tensor.matmul_mx(
                out=acc[:],
                lhsT=wa_codes[b][:, cols].bitcast(FP8X4),
                lhsT_scale=wa_scales[b][:, cols],
                rhs=v_codes[half][:].bitcast(FP8X4),
                rhs_scale=v_scales[half][:],
                start=True,
                stop=True,
            )
            projections[i] = rows_tile(f"projection{i}", tag)
            nc.scalar.copy(out=projections[i][:], in_=acc[:])

        def modulate(i, phase, sine):
            b, t, half = STEPS[i]
            if t == 0:
                h_rows[b, half] = keep.tile([P, PACK, HALF], BF16, name=f"h_rows{b}{half}", align_bytes=ALIGN)
            window = freq[PACK * b + t][:].indirect(half_list(half))
            nc.vector.tensor_tensor(out=phase, in0=window, in1=projections[i][:], op=MULT)
            nc.scalar.activation(out=sine, in_=phase, func=SIN)
            scale_rows(i < len(STEPS) - 3, h_rows[b, half][:, t, :], sine, gain_sb[:, b, t : t + 1])

        def quantise_h(b, half, tag):
            woven = keep.tile([P, HALF, PACK], BF16, name=f"h_woven{b}{half}", tag=tag, align_bytes=ALIGN)
            quantise(weave(woven, h_rows[b, half]), h_codes[b, half][:], h_scales[b, half][:])

        def ring_sine():
            return ring.tile([P, HALF], F32, name="sine")[:]

        y_rows = {}
        y_codes = {}
        y_out = out_0.rearrange("(g p t) j -> g p t j", g=GROUPS, t=PACK)

        def output_slice(g, t, half, sine):
            if t == 0:
                y_rows[g, half] = big_tile(f"y_rows{g}{half}")
            acc = psum.tile([P, HALF], F32, name="acc")
            col = GROUP * g + P * t
            for b in range(GROUPS):
                nc.tensor.matmul_mx(
                    out=acc[:],
                    lhsT=w4_codes[:, b, 2 * col : 2 * (col + P)].bitcast(FP4X4),
                    lhsT_scale=w4_dealt_scales[b][:, col : col + P],
                    rhs=h_codes[b, half][:].bitcast(FP8X4),
                    rhs_scale=h_scales[b, half][:],
                    start=(b == 0),
                    stop=(b == GROUPS - 1),
                )
            nc.scalar.activation(out=sine, in_=acc[:], func=SIN)
            on_scalar = t == PACK - 1 or ((g, half) == (0, 0) and t < 2)
            scale_rows(on_scalar, y_rows[g, half][:, t, :], sine, amp_sb[:, g, t : t + 1])
            if t % 2:
                nc.sync.dma_start(
                    out=y_out[g, :, t - 1 : t + 1, HALF * half : HALF * (half + 1)],
                    in_=y_rows[g, half][:, t - 1 : t + 1, :],
                )

        def quantise_y(g, half):
            y_codes[g, half] = twin.tile([P, HALF], U32, name="y_codes", align_bytes=ALIGN, bufs=3)
            woven = twin.tile([P, HALF, PACK], BF16, name="y_woven", tag="woven", align_bytes=ALIGN)
            scales = y_scales[:, g, HALF * half : HALF * (half + 1)]
            quantise(weave(woven, y_rows[g, half]), y_codes[g, half][:], scales)

        def store_codes(g, half):
            words = out_1[g].rearrange("p m t -> p (m t)").bitcast(I32)
            nc.sync.dma_start(out=words[:, HALF * half : HALF * (half + 1)], in_=y_codes[g, half][:].bitcast(I32))

        look_up_codes(0)
        quantise(weave_wa(0, nc.scalar.copy), wa_codes[0][:], wa_scales[0][:])
        look_up_codes(1)
        for i in range(AHEAD):
            project(i, f"slot{i}")
        for i in range(PIVOT + 1):
            if STEPS[i] == (0, 1, 1):
                quantise(weave_wa(1, nc.vector.tensor_copy), wa_codes[1][:], wa_scales[1][:])
            project(i + AHEAD, f"slot{i + AHEAD}")
            inherits = i >= AHEAD and i - AHEAD != WEAVE_00_AFTER
            phase = rows_tile(f"phase{i}", f"slot{i - AHEAD}" if inherits else f"phase{i}")
            modulate(i, phase[:], rows_tile("pivot_sine", "pivot_sine")[:] if i == PIVOT else ring_sine())
            if STEPS[i] == (0, PACK - 1, 1):
                deal_w4()
            if i == WEAVE_00_AFTER:
                quantise_h(0, 0, f"slot{i}")
        quantise_h(1, 0, "h_woven10")

        first, second, third, fourth = range(PIVOT + 1, len(STEPS))
        project(third, f"phase{PIVOT}")
        early_phases = rows_tile("early_phases", f"slot{PIVOT}", rows=2)
        early_sines = rows_tile("early_sines", "pivot_sine", rows=2)
        modulate(first, early_phases[:, 0, :], early_sines[:, 0, :])
        modulate(second, early_phases[:, 1, :], early_sines[:, 1, :])
        project(fourth, f"slot{PIVOT}")
        output_slice(0, 0, 0, ring_sine())
        output_slice(0, 1, 0, rows_tile("slice_1_sine", "last_sine")[:])
        late_phases = rows_tile("late_phases", "h_rows10", rows=2)
        modulate(third, late_phases[:, 0, :], ring_sine())
        quantise_h(0, 1, f"phase{PIVOT}")
        output_slice(0, 2, 0, ring_sine())
        modulate(fourth, late_phases[:, 1, :], rows_tile("last_sine", "last_sine")[:])
        output_slice(0, 3, 0, ring_sine())
        quantise_h(1, 1, "h_woven11")

        quarters = [(g, half) for half in range(2) for g in range(GROUPS)]
        for n in range(1, len(quarters)):
            g, half = quarters[n]
            for t in range(PACK):
                output_slice(g, t, half, ring_sine())
            if n >= 2:
                store_codes(*quarters[n - 2])
            quantise_y(*quarters[n - 1])
        quantise_y(*quarters[-1])
        store_codes(*quarters[-2])
        store_codes(*quarters[-1])
        for q in range(QUADRANTS):
            nc.sync.dma_start(
                out=out_2[:, 4 * q : 4 * q + 4, :].rearrange("g q c -> q g c").bitcast(I32),
                in_=y_scales[32 * q : 32 * q + 4].bitcast(I32),
            )
